import numpy as np
import ml_dtypes


def mxq(x, axis, fmt="e4m3"):
    dtype, down = {"e4m3": (ml_dtypes.float8_e4m3fn, 7), "e5m2": (ml_dtypes.float8_e5m2, 14)}[fmt]
    v = np.moveaxis(np.asarray(x, np.float32).astype(ml_dtypes.bfloat16).astype(np.float64), axis, -1)
    blocks = v.reshape(v.shape[:-1] + (-1, 32))
    amax = np.abs(blocks).max(-1, keepdims=True)
    byte = np.maximum(np.where(amax > 0, np.frexp(amax)[1] - 1 + 127, 0) - down, 1)
    scale = np.exp2(byte - 127.0)
    codes = (blocks / scale).astype(np.float32).astype(dtype).astype(np.float64)
    return np.moveaxis((codes * scale).reshape(v.shape), -1, axis)


WIDE = False


def mx_kscale(k):
    if not WIDE:
        return np.ones(k)
    levels = np.array([10, -10, 5, -5, 0])
    if k % 512:
        return np.exp2(np.random.permutation(np.resize(levels, k // 32))).repeat(32)
    a = np.empty((k // 512, 16))
    for p in range(k // 512):
        a[p, :8] = np.random.permutation(np.resize(levels, 8))
        for g in range(8):
            far = levels[np.abs(levels - a[p, g]) >= 10]
            a[p, g + 8] = far[np.random.randint(len(far))]
    return np.exp2(a.ravel()).repeat(32)


def f64(x):
    return np.asarray(x).astype(np.float64)


def striped(idx):
    return np.tile(idx.reshape(-1, 16).T, (8, 1)).astype(np.uint16)


def unstriped(offs):
    return offs[:16].T.reshape(-1).astype(np.int64)


E2M1 = np.array([0.0, 0.5, 1.0, 1.5, 2.0, 3.0, 4.0, 6.0, -0.0, -0.5, -1.0, -1.5, -2.0, -3.0, -4.0, -6.0])


def pack_weight(w, fmt):
    k, n = w.shape
    w = f64(np.asarray(w, np.float32).astype(ml_dtypes.bfloat16)).reshape(k // 32, 32, n)
    amax = np.abs(w).max(1)
    if fmt == "e4m3":
        byte = np.frexp(amax)[1] - 1 + 127 - 7
    else:
        mant, ex = np.frexp(amax / 6.0)
        byte = np.where(mant > 0.5, ex, ex - 1) + 127
    byte = np.clip(np.where(amax > 0, byte, 1), 1, 254)
    scaled = (w * np.exp2(127.0 - byte)[:, None, :]).reshape(k, n).astype(np.float32)
    by_word = np.ascontiguousarray(scaled.reshape(k // 512, 128, 4, n).transpose(0, 1, 3, 2))
    if fmt == "e4m3":
        words = by_word.astype(ml_dtypes.float8_e4m3fn).view(np.uint8)
    else:
        c = by_word.astype(ml_dtypes.float4_e2m1fn).view(np.uint8) & 0xF
        words = (c[..., 0::2] | (c[..., 1::2] << 4)).reshape(k // 512, 128, 2 * n)
    return np.ascontiguousarray(words), np.ascontiguousarray(byte.astype(np.uint8).reshape(k // 512, 16, n))


def unpack_weight(words, scales, fmt):
    g, _, n = scales.shape
    words = np.ascontiguousarray(words).reshape(g, 128, n, -1)
    if fmt == "e4m3":
        vals = words.view(ml_dtypes.float8_e4m3fn).astype(np.float64)
    else:
        nib = np.empty((g, 128, n, 4), np.uint8)
        nib[..., 0::2] = words & 0xF
        nib[..., 1::2] = words >> 4
        vals = E2M1[nib]
    vals = vals * np.repeat(np.exp2(scales.astype(np.float64) - 127.0), 8, axis=1)[..., None]
    return vals.transpose(0, 1, 3, 2).reshape(g * 512, n)


def gelu(v):
    return 0.5 * v * (1.0 + np.tanh(np.sqrt(2.0 / np.pi) * (v + 0.044715 * v**3)))


K, H, T, S, S2, T3, P = 1536, 512, 2048, 1024, 1024, 2048, 512

def setup_inputs():
    n = np.random.standard_normal
    s = mx_kscale(K)[:, None]
    u = mx_kscale(H)[:, None]
    d = {}
    d["tab_words"], d["tab_scales"] = pack_weight(n((K, T)) * s, "e4m3")
    d["offs"] = striped(np.random.permutation(T)[:S])
    d["w1"] = (n((K, H)) / K ** 0.5 / s).astype(np.float32)
    d["w4_words"], d["w4_scales"] = pack_weight(n((K, H)) / K ** 0.5 / s, "e2m1")
    d["level"] = (0.8 * n(S)).astype(np.float32)
    d["gain"] = (np.exp(0.3 * n(H)) * u[:, 0]).astype(np.float32)
    d["tab2_words"], d["tab2_scales"] = pack_weight(n((H, T3)) / H ** 0.5 / u, "e4m3")
    d["offs2"] = striped(np.random.permutation(T3)[:S2])
    d["shift"] = (0.7 * n(S2)).astype(np.float32)
    d["pos1"] = striped(np.random.permutation(S)[:P])
    d["pos2"] = striped(np.random.permutation(S)[:P])
    return d

def reference(tab_words, tab_scales, offs, w1, w4_words, w4_scales, level, gain,
              tab2_words, tab2_scales, offs2, shift, pos1, pos2):
    v = unpack_weight(tab_words, tab_scales, "e4m3")[:, unstriped(offs)]
    w4 = unpack_weight(w4_words, w4_scales, "e2m1")
    upper = mxq(f64(w1), 0, "e4m3").T @ v
    lower = w4.T @ v
    lev = f64(level)[None, :]
    h = f64(gain)[:, None] * (np.maximum(upper, lev) + np.minimum(lower, lev))
    hq = mxq(h, 0, "e4m3")
    v2 = unpack_weight(tab2_words, tab2_scales, "e4m3")[:, unstriped(offs2)]
    e = v2.T @ hq
    arrival = np.abs(e[:, unstriped(pos1)] + f64(shift)[:, None])
    return arrival * e[:, unstriped(pos2)]

@@ -1,0 +1,237 @@
+from contextlib import ExitStack
+
+import concourse.mybir as mybir
+from concourse.masks import make_identity
+
+K, H, T, S, S2, T3, NP = 1536, 512, 2048, 1024, 1024, 2048, 512
+FLOPS = 2 * (2 * K * H * S + H * S2 * S)
+
+F32 = mybir.dt.float32
+BF16 = mybir.dt.bfloat16
+I32 = mybir.dt.int32
+U32 = mybir.dt.uint32
+U16 = mybir.dt.uint16
+U8 = mybir.dt.uint8
+FP8X4 = mybir.dt.float8_e4m3fn_x4
+FP4X4 = mybir.dt.float4_e2m1fn_x4
+ALU = mybir.AluOpType
+ACT = mybir.ActivationFunctionType
+
+P = 128
+PASSES = K // 512
+JT = S // P
+MT = S2 // P
+HALF = 512
+LIVE0 = 32 - 4 * PASSES
+
+
+def tile_list_ripening_schedule_scores_kernel(
+    tc, tab_words, tab_scales, offs, w1, w4_words, w4_scales, level, gain,
+    tab2_words, tab2_scales, offs2, shift, pos1, pos2, out,
+):
+    nc = tc.nc
+    with ExitStack() as ctx:
+        keep = ctx.enter_context(tc.tile_pool(name="keep", bufs=1))
+        ring = ctx.enter_context(tc.tile_pool(name="ring", bufs=3))
+        stage = ctx.enter_context(tc.tile_pool(name="stage", bufs=3))
+        psum = ctx.enter_context(tc.psum_pool(name="psum", bufs=1))
+        banks = [psum.tile([P, 512], F32, name="bank%d" % b) for b in range(8)]
+
+        offs_sb = keep.tile([P, S // 16], U16, name="offs_sb")
+        offs2_sb = keep.tile([P, S2 // 16], U16, name="offs2_sb")
+        pos1_sb = keep.tile([P, NP // 16], U16, name="pos1_sb")
+        pos2_sb = keep.tile([P, NP // 16], U16, name="pos2_sb")
+
+        tab_sc = keep.tile([P, T], U8, name="tab_sc", align_bytes=64)
+        tab2_sc = keep.tile([P, T3], U8, name="tab2_sc", align_bytes=64)
+        w4_sc = keep.tile([P, PASSES, H], U8, name="w4_sc", align_bytes=64)
+        w4_w = keep.tile([P, PASSES, 2 * H], U8, name="w4_w", align_bytes=64)
+        v_sc = [keep.tile([P, S], U8, name="v_sc%d" % a, align_bytes=64) for a in range(PASSES)]
+        rows = keep.tile([P, P], F32, name="rows")
+        ident = keep.tile([P, P], F32, name="ident")
+        gain_sb = keep.tile([P, 4], F32, name="gain_sb")
+
+        nc.vector.memset(w4_sc[:].rearrange("p a n -> p (a n)").bitcast(I32), 0)
+        for q in range(4):
+            nc.vector.memset(tab_sc[32 * q : 32 * q + LIVE0, :].bitcast(I32), 0)
+
+        def load_words(words, name):
+            win = stage.tile([P, T], U32, name=name, tag="stage", align_bytes=64)
+            nc.sync.dma_start(out=win[:].bitcast(I32), in_=words.rearrange("p t i -> p (t i)").bitcast(I32))
+            return win
+
+        nc.sync.dma_start(offs_sb[:], offs)
+        for q, queue in enumerate((nc.scalar, nc.sync, nc.scalar, nc.sync)):
+            queue.dma_start(
+                out=tab_sc[32 * q + LIVE0 : 32 * (q + 1), :].bitcast(I32),
+                in_=tab_scales[:, 4 * q : 4 * q + 4, :].bitcast(I32),
+            )
+        nc.gpsimd.memset(rows[:], 0.0)
+        for a in range(PASSES):
+            nc.gpsimd.memset(v_sc[a][96:128, :].bitcast(I32), 0)
+        nc.gpsimd.memset(tab2_sc[:].bitcast(I32), 0)
+        tab_w = [load_words(tab_words[0], "tab_w0")]
+        nc.sync.dma_start(offs2_sb[:], offs2)
+        nc.sync.dma_start(pos1_sb[:], pos1)
+        nc.sync.dma_start(pos2_sb[:], pos2)
+        nc.sync.dma_start(out=w4_w[:].bitcast(I32), in_=w4_words.rearrange("a p n -> p a n").bitcast(I32))
+        for a in range(1, PASSES):
+            tab_w.append(load_words(tab_words[a], "tab_w%d" % a))
+        for q in range(4):
+            nc.scalar.dma_start(
+                out=w4_sc[32 * q : 32 * q + 4, :, :].bitcast(I32),
+                in_=w4_scales[:, 4 * q : 4 * q + 4, :].rearrange("a r n -> r a n").bitcast(I32),
+            )
+        nc.scalar.dma_start(out=rows[0:JT, :], in_=level.rearrange("(t p) -> t p", p=P))
+        nc.gpsimd.dma_start(out=rows[JT : JT + MT, :], in_=shift.rearrange("(t p) -> t p", p=P))
+        make_identity(nc, ident[:])
+        for q in range(4):
+            nc.gpsimd.dma_start(
+                out=tab2_sc[32 * q : 32 * q + 4, :].bitcast(I32),
+                in_=tab2_scales[0, 4 * q : 4 * q + 4, :].bitcast(I32),
+            )
+        nc.gpsimd.dma_start(out=gain_sb[:], in_=gain.rearrange("(p t) -> p t", t=4))
+        w1_raw = []
+        for a in range(PASSES):
+            raw = stage.tile([P, 4, H], F32, name="w1_raw%d" % a, tag="stage", align_bytes=64)
+            nc.sync.dma_start(out=raw[:], in_=w1[512 * a : 512 * (a + 1), :].rearrange("(p i) c -> p i c", i=4))
+            w1_raw.append(raw)
+        tab2_w = load_words(tab2_words[0], "tab2_w")
+
+        v_packed = keep.tile([P, S], U8, name="v_packed", align_bytes=64)
+        nc.vector.tensor_copy(v_packed[:], tab_sc[:].indirect(offs_sb[:]))
+        for a in range(PASSES):
+            first = LIVE0 + 4 * a
+            nc.scalar.dma_start(out=v_sc[a][0:100, :].bitcast(I32), in_=v_packed[first : first + 100, :].bitcast(I32))
+
+        nc.tensor.transpose(banks[7][:, 0:P], rows[:], ident[:])
+        cols = keep.tile([P, JT + MT], F32, name="cols")
+        neg_level = keep.tile([P, JT], F32, name="neg_level")
+        nc.scalar.copy(cols[:], banks[7][:, 0 : JT + MT])
+        nc.scalar.activation(neg_level[:], banks[7][:, 0:JT], ACT.Copy, scale=-1.0)
+
+        v_w = [[keep.tile([P, HALF], U32, name="v_w%d_%d" % (a, h), align_bytes=64) for h in range(2)] for a in range(PASSES)]
+
+        def v_operand(a, jt):
+            h, c = divmod(jt * P, HALF)
+            return v_w[a][h][:, c : c + P].bitcast(FP8X4), v_sc[a][:, jt * P : (jt + 1) * P]
+
+        for a in range(PASSES):
+            for h in range(2):
+                nc.vector.tensor_copy(v_w[a][h][:], tab_w[a][:].indirect(offs_sb[:, 32 * h : 32 * (h + 1)]))
+            for jt in range(JT):
+                words, scales = v_operand(a, jt)
+                nc.tensor.matmul_mx(
+                    out=banks[jt][:], lhsT=words, lhsT_scale=scales,
+                    rhs=w4_w[:, a, :].bitcast(FP4X4), rhs_scale=w4_sc[:, a, :],
+                    start=(a == 0), stop=(a == PASSES - 1),
+                )
+
+        v2_sc = keep.tile([P, S2], U8, name="v2_sc", align_bytes=64)
+        nc.vector.tensor_copy(v2_sc[:], tab2_sc[:].indirect(offs2_sb[:]))
+
+        low = []
+        for jt in range(JT):
+            t_low = keep.tile([P, 4, P], F32, name="low%d" % jt)
+            nc.vector.tensor_scalar(
+                out=t_low[:], in0=banks[jt][:].rearrange("p (q t) -> p t q", t=4),
+                scalar1=cols[:, jt : jt + 1], scalar2=cols[:, jt : jt + 1], op0=ALU.min, op1=ALU.add,
+            )
+            low.append(t_low)
+
+        for a in range(PASSES):
+            grouped = keep.tile([P, H, 4], BF16, name="w1_bf%d" % a, align_bytes=64)
+            nc.scalar.copy(
+                grouped[:].rearrange("p (c n) i -> p c i n", n=4),
+                w1_raw[a][:].rearrange("p i (c n) -> p c i n", n=4),
+            )
+            codes = keep.tile([P, H], U32, name="w1_codes%d" % a, align_bytes=64)
+            plane = keep.tile([P, H], U8, name="w1_plane%d" % a, align_bytes=64)
+            nc.vector.quantize_mx(out=codes[:].bitcast(FP8X4), scales=plane[:], in_=grouped[:].rearrange("p c i -> p (c i)"))
+            for jt in range(JT):
+                words, scales = v_operand(a, jt)
+                nc.tensor.matmul_mx(
+                    out=banks[jt][:], lhsT=words, lhsT_scale=scales,
+                    rhs=codes[:].bitcast(FP8X4), rhs_scale=plane[:],
+                    start=(a == 0), stop=(a == PASSES - 1),
+                )
+
+        v2_w = [keep.tile([P, 2 * P], U32, name="v2_w%d" % i, align_bytes=64) for i in range(MT // 2)]
+
+        def gather_v2(i):
+            nc.vector.tensor_copy(v2_w[i][:], tab2_w[:].indirect(offs2_sb[:, 16 * i : 16 * (i + 1)]))
+
+        gather_v2(0)
+
+        h_codes = [keep.tile([P, HALF], U32, name="h_codes%d" % h, align_bytes=64) for h in range(2)]
+        h_plane = [keep.tile([P, HALF], U8, name="h_plane%d" % h, align_bytes=64) for h in range(2)]
+        h_bf = []
+
+        def quantise_h(jt):
+            h, c = divmod(jt * P, HALF)
+            nc.vector.quantize_mx(
+                out=h_codes[h][:, c : c + P].bitcast(FP8X4), scales=h_plane[h][:, c : c + P],
+                in_=h_bf[jt][:].rearrange("p j t -> p (j t)"),
+            )
+
+        ups = []
+        for jt in range(JT):
+            up = keep.tile([P, 4, P], F32, name="up%d" % jt)
+            nc.scalar.activation(
+                up[:], banks[jt][:].rearrange("p (q t) -> p t q", t=4), ACT.Relu,
+                bias=neg_level[:, jt : jt + 1], scale=1.0,
+            )
+            ups.append(up)
+        for jt in range(JT):
+            for t in range(4):
+                dst = banks[jt][:, t * P : (t + 1) * P]
+                nc.tensor.matmul(dst, lhsT=low[jt][:, t, :], rhs=ident[:], start=True, stop=False, is_transpose=True)
+                nc.tensor.matmul(dst, lhsT=ups[jt][:, t, :], rhs=ident[:], start=False, stop=True, is_transpose=True)
+            hb = keep.tile([P, P, 4], BF16, name="h_bf%d" % jt, align_bytes=64)
+            nc.vector.tensor_tensor(
+                out=hb[:], in0=banks[jt][:].rearrange("p (t j) -> p j t", t=4),
+                in1=gain_sb[:].unsqueeze(1).to_broadcast([P, P, 4]), op=ALU.mult,
+            )
+            h_bf.append(hb)
+            if jt > 0:
+                quantise_h(jt - 1)
+        quantise_h(JT - 1)
+
+        scores = {}
+        arrival = {}
+
+        def make_scores(m):
+            e = ring.tile([P, S], F32, name="e", bufs=4)
+            for h in range(2):
+                bank = banks[(2 * m + h) % 8]
+                nc.tensor.matmul_mx(
+                    out=bank[:], lhsT=v2_w[m // 2][:, (m % 2) * P : (m % 2 + 1) * P].bitcast(FP8X4),
+                    lhsT_scale=v2_sc[:, m * P : (m + 1) * P],
+                    rhs=h_codes[h][:].bitcast(FP8X4), rhs_scale=h_plane[h][:], start=True, stop=True,
+                )
+                nc.scalar.copy(e[:, h * HALF : (h + 1) * HALF], bank[:])
+            scores[m] = e
+
+        def pick_first(m):
+            picked = ring.tile([P, NP], F32, name="picked")
+            nc.vector.tensor_copy(picked[:], scores[m][:].indirect(pos1_sb[:]))
+            arr = ring.tile([P, NP], F32, name="arr")
+            nc.scalar.activation(arr[:], picked[:], ACT.Abs, bias=cols[:, JT + m : JT + m + 1], scale=1.0)
+            arrival[m] = arr
+
+        def pick_second(m):
+            res = ring.tile([P, NP], F32, name="res")
+            nc.vector.tensor_tensor(res[:], scores[m][:].indirect(pos2_sb[:]), arrival[m][:], ALU.mult)
+            nc.sync.dma_start(out=out[m * P : (m + 1) * P, :], in_=res[:])
+
+        make_scores(0)
+        make_scores(1)
+        pick_first(0)
+        for m in range(MT):
+            if m + 2 < MT:
+                if m % 2 == 0:
+                    gather_v2(m // 2 + 1)
+                make_scores(m + 2)
+            if m + 1 < MT:
+                pick_first(m + 1)
+            pick_second(m)

@@ -22,7 +22,7 @@ PASSES = K // 512
 JT = S // P
 MT = S2 // P
 HALF = 512
-LIVE0 = 32 - 4 * PASSES
+SCALAR_COLUMNS = (256, 128, 256)
 
 
 def tile_list_ripening_schedule_scores_kernel(
@@ -33,7 +33,7 @@ def tile_list_ripening_schedule_scores_kernel(
     with ExitStack() as ctx:
         keep = ctx.enter_context(tc.tile_pool(name="keep", bufs=1))
         ring = ctx.enter_context(tc.tile_pool(name="ring", bufs=3))
-        stage = ctx.enter_context(tc.tile_pool(name="stage", bufs=3))
+        shared = ctx.enter_context(tc.tile_pool(name="shared", bufs=1))
         psum = ctx.enter_context(tc.psum_pool(name="psum", bufs=1))
         banks = [psum.tile([P, 512], F32, name="bank%d" % b) for b in range(8)]
 
@@ -42,7 +42,7 @@ def tile_list_ripening_schedule_scores_kernel(
         pos1_sb = keep.tile([P, NP // 16], U16, name="pos1_sb")
         pos2_sb = keep.tile([P, NP // 16], U16, name="pos2_sb")
 
-        tab_sc = keep.tile([P, T], U8, name="tab_sc", align_bytes=64)
+        tab_sc = keep.tile([P, T], U8, name="tab_sc", tag="tab_sc", align_bytes=64)
         tab2_sc = keep.tile([P, T3], U8, name="tab2_sc", align_bytes=64)
         w4_sc = keep.tile([P, PASSES, H], U8, name="w4_sc", align_bytes=64)
         w4_w = keep.tile([P, PASSES, 2 * H], U8, name="w4_w", align_bytes=64)
@@ -51,38 +51,46 @@ def tile_list_ripening_schedule_scores_kernel(
         ident = keep.tile([P, P], F32, name="ident")
         gain_sb = keep.tile([P, 4], F32, name="gain_sb")
 
-        nc.vector.memset(w4_sc[:].rearrange("p a n -> p (a n)").bitcast(I32), 0)
-        for q in range(4):
-            nc.vector.memset(tab_sc[32 * q : 32 * q + LIVE0, :].bitcast(I32), 0)
-
-        def load_words(words, name):
-            win = stage.tile([P, T], U32, name=name, tag="stage", align_bytes=64)
-            nc.sync.dma_start(out=win[:].bitcast(I32), in_=words.rearrange("p t i -> p (t i)").bitcast(I32))
-            return win
-
-        nc.sync.dma_start(offs_sb[:], offs)
-        for q, queue in enumerate((nc.scalar, nc.sync, nc.scalar, nc.sync)):
-            queue.dma_start(
-                out=tab_sc[32 * q + LIVE0 : 32 * (q + 1), :].bitcast(I32),
-                in_=tab_scales[:, 4 * q : 4 * q + 4, :].bitcast(I32),
-            )
+        nc.gpsimd.memset(tab_sc[:, 0 : T // 2].bitcast(I32), 0)
+        nc.vector.memset(tab_sc[:, T // 2 : T].bitcast(I32), 0)
         nc.gpsimd.memset(rows[:], 0.0)
-        for a in range(PASSES):
-            nc.gpsimd.memset(v_sc[a][96:128, :].bitcast(I32), 0)
-        nc.gpsimd.memset(tab2_sc[:].bitcast(I32), 0)
-        tab_w = [load_words(tab_words[0], "tab_w0")]
-        nc.sync.dma_start(offs2_sb[:], offs2)
-        nc.sync.dma_start(pos1_sb[:], pos1)
-        nc.sync.dma_start(pos2_sb[:], pos2)
-        nc.sync.dma_start(out=w4_w[:].bitcast(I32), in_=w4_words.rearrange("a p n -> p a n").bitcast(I32))
+        nc.vector.memset(w4_sc[:].rearrange("p a n -> p (a n)").bitcast(I32), 0)
         for a in range(1, PASSES):
-            tab_w.append(load_words(tab_words[a], "tab_w%d" % a))
-        for q in range(4):
-            nc.scalar.dma_start(
+            nc.vector.memset(v_sc[a][96:128, :].bitcast(I32), 0)
+        nc.vector.memset(tab2_sc[:].bitcast(I32), 0)
+
+        def load_words(win, words):
+            nc.sync.dma_start(out=win[:].bitcast(I32), in_=words.rearrange("p t i -> p (t i)").bitcast(I32))
+
+        def load_w4_scales(q):
+            nc.sync.dma_start(
                 out=w4_sc[32 * q : 32 * q + 4, :, :].bitcast(I32),
                 in_=w4_scales[:, 4 * q : 4 * q + 4, :].rearrange("a r n -> r a n").bitcast(I32),
             )
-        nc.scalar.dma_start(out=rows[0:JT, :], in_=level.rearrange("(t p) -> t p", p=P))
+
+        tab_w = [
+            shared.tile([P, T], U32, name="tab_w0", offset=2 * T),
+            keep.tile([P, T], U32, name="tab_w1", tag="stage1", align_bytes=64),
+            shared.tile([P, T], U32, name="tab_w2", offset=8 * T + HALF),
+        ]
+        nc.sync.dma_start(offs_sb[:], offs)
+        nc.sync.dma_start(offs2_sb[:], offs2)
+        nc.sync.dma_start(pos1_sb[:], pos1)
+        load_words(tab_w[0], tab_words[0])
+        for q, queue in enumerate((nc.scalar, nc.sync, nc.scalar, nc.sync)):
+            queue.dma_start(
+                out=tab_sc[32 * q : 32 * q + 4 * PASSES, :].bitcast(I32),
+                in_=tab_scales[:, 4 * q : 4 * q + 4, :].bitcast(I32),
+            )
+        load_w4_scales(0)
+        load_w4_scales(1)
+        nc.sync.dma_start(out=w4_w[:].bitcast(I32), in_=w4_words.rearrange("a p n -> p a n").bitcast(I32))
+        load_w4_scales(2)
+        load_w4_scales(3)
+        load_words(tab_w[1], tab_words[1])
+        load_words(tab_w[2], tab_words[2])
+        nc.sync.dma_start(pos2_sb[:], pos2)
+        nc.gpsimd.dma_start(out=rows[0:JT, :], in_=level.rearrange("(t p) -> t p", p=P))
         nc.gpsimd.dma_start(out=rows[JT : JT + MT, :], in_=shift.rearrange("(t p) -> t p", p=P))
         make_identity(nc, ident[:])
         for q in range(4):
@@ -91,26 +99,43 @@ def tile_list_ripening_schedule_scores_kernel(
                 in_=tab2_scales[0, 4 * q : 4 * q + 4, :].bitcast(I32),
             )
         nc.gpsimd.dma_start(out=gain_sb[:], in_=gain.rearrange("(p t) -> p t", t=4))
-        w1_raw = []
-        for a in range(PASSES):
-            raw = stage.tile([P, 4, H], F32, name="w1_raw%d" % a, tag="stage", align_bytes=64)
-            nc.sync.dma_start(out=raw[:], in_=w1[512 * a : 512 * (a + 1), :].rearrange("(p i) c -> p i c", i=4))
-            w1_raw.append(raw)
-        tab2_w = load_words(tab2_words[0], "tab2_w")
 
-        v_packed = keep.tile([P, S], U8, name="v_packed", align_bytes=64)
-        nc.vector.tensor_copy(v_packed[:], tab_sc[:].indirect(offs_sb[:]))
-        for a in range(PASSES):
-            first = LIVE0 + 4 * a
-            nc.scalar.dma_start(out=v_sc[a][0:100, :].bitcast(I32), in_=v_packed[first : first + 100, :].bitcast(I32))
+        v_w = [
+            [
+                keep.tile(
+                    [P, HALF], U32, name="v_w%d_%d" % (a, h),
+                    tag="tab_sc" if (a, h) == (0, 1) else "v_w%d_%d" % (a, h), align_bytes=64,
+                )
+                for h in range(2)
+            ]
+            for a in range(PASSES)
+        ]
+
+        def gather_v(a, h):
+            nc.vector.tensor_copy(v_w[a][h][:], tab_w[a][:].indirect(offs_sb[:, 32 * h : 32 * (h + 1)]))
+
+        gather_v(0, 0)
+        for h in range(2):
+            nc.vector.tensor_copy(
+                v_sc[0][:, h * HALF : (h + 1) * HALF], tab_sc[:].indirect(offs_sb[:, 32 * h : 32 * (h + 1)])
+            )
+        for a in range(1, PASSES):
+            nc.sync.dma_start(out=v_sc[a][0:112, :].bitcast(I32), in_=v_sc[0][4 * a : 4 * a + 112, :].bitcast(I32))
+
+        w1_raw = [
+            shared.tile([P, 4, H], F32, name="w1_raw0", offset=0),
+            shared.tile([P, 4, H], F32, name="w1_raw1", offset=4 * T),
+            keep.tile([P, 4, H], F32, name="w1_raw2", tag="stage1", align_bytes=64),
+        ]
+        tab2_w = shared.tile([P, T3], U32, name="tab2_w", offset=8 * T)
 
         nc.tensor.transpose(banks[7][:, 0:P], rows[:], ident[:])
         cols = keep.tile([P, JT + MT], F32, name="cols")
         neg_level = keep.tile([P, JT], F32, name="neg_level")
         nc.scalar.copy(cols[:], banks[7][:, 0 : JT + MT])
         nc.scalar.activation(neg_level[:], banks[7][:, 0:JT], ACT.Copy, scale=-1.0)
-
-        v_w = [[keep.tile([P, HALF], U32, name="v_w%d_%d" % (a, h), align_bytes=64) for h in range(2)] for a in range(PASSES)]
+        twice_level = keep.tile([P, JT], F32, name="twice_level")
+        nc.scalar.activation(twice_level[:], banks[7][:, 0:JT], ACT.Copy, scale=2.0)
 
         def v_operand(a, jt):
             h, c = divmod(jt * P, HALF)
@@ -118,7 +143,8 @@ def tile_list_ripening_schedule_scores_kernel(
 
         for a in range(PASSES):
             for h in range(2):
-                nc.vector.tensor_copy(v_w[a][h][:], tab_w[a][:].indirect(offs_sb[:, 32 * h : 32 * (h + 1)]))
+                if (a, h) != (0, 0):
+                    gather_v(a, h)
             for jt in range(JT):
                 words, scales = v_operand(a, jt)
                 nc.tensor.matmul_mx(
@@ -127,39 +153,91 @@ def tile_list_ripening_schedule_scores_kernel(
                     start=(a == 0), stop=(a == PASSES - 1),
                 )
 
-        v2_sc = keep.tile([P, S2], U8, name="v2_sc", align_bytes=64)
-        nc.vector.tensor_copy(v2_sc[:], tab2_sc[:].indirect(offs2_sb[:]))
-
-        low = []
-        for jt in range(JT):
-            t_low = keep.tile([P, 4, P], F32, name="low%d" % jt)
-            nc.vector.tensor_scalar(
-                out=t_low[:], in0=banks[jt][:].rearrange("p (q t) -> p t q", t=4),
-                scalar1=cols[:, jt : jt + 1], scalar2=cols[:, jt : jt + 1], op0=ALU.min, op1=ALU.add,
-            )
-            low.append(t_low)
-
         for a in range(PASSES):
-            grouped = keep.tile([P, H, 4], BF16, name="w1_bf%d" % a, align_bytes=64)
-            nc.scalar.copy(
-                grouped[:].rearrange("p (c n) i -> p c i n", n=4),
-                w1_raw[a][:].rearrange("p i (c n) -> p c i n", n=4),
+            nc.sync.dma_start(
+                out=w1_raw[a][:], in_=w1[512 * a : 512 * (a + 1), :].rearrange("(p i) c -> p i c", i=4)
             )
-            codes = keep.tile([P, H], U32, name="w1_codes%d" % a, align_bytes=64)
-            plane = keep.tile([P, H], U8, name="w1_plane%d" % a, align_bytes=64)
-            nc.vector.quantize_mx(out=codes[:].bitcast(FP8X4), scales=plane[:], in_=grouped[:].rearrange("p c i -> p (c i)"))
-            for jt in range(JT):
-                words, scales = v_operand(a, jt)
-                nc.tensor.matmul_mx(
-                    out=banks[jt][:], lhsT=words, lhsT_scale=scales,
-                    rhs=codes[:].bitcast(FP8X4), rhs_scale=plane[:],
-                    start=(a == 0), stop=(a == PASSES - 1),
+        load_words(tab2_w, tab2_words[0])
+
+        w1_bf, w1_codes, w1_plane, low = [], [], [], []
+
+        def round_w1(a):
+            grouped = keep.tile([P, H, 4], BF16, name="w1_bf%d" % a, tag="w1_bf%d" % a, align_bytes=64)
+
+            def by_fours(c0, c1):
+                return (
+                    grouped[:, c0:c1, :].rearrange("p (c n) i -> p c i n", n=4),
+                    w1_raw[a][:, :, c0:c1].rearrange("p i (c n) -> p c i n", n=4),
                 )
 
-        v2_w = [keep.tile([P, 2 * P], U32, name="v2_w%d" % i, align_bytes=64) for i in range(MT // 2)]
+            split = SCALAR_COLUMNS[a]
+            nc.scalar.copy(*by_fours(0, split))
+            for c in range(split, H, P):
+                nc.gpsimd.tensor_scalar(
+                    out=grouped[:, c : c + P, :], in0=w1_raw[a][:, :, c : c + P].rearrange("p i c -> p c i"),
+                    scalar1=1.0, scalar2=0.0, op0=ALU.mult, op1=ALU.add,
+                )
+            w1_bf.append(grouped)
+
+        def quantise_w1(a):
+            codes = keep.tile([P, H], U32, name="w1_codes%d" % a, align_bytes=64)
+            plane = keep.tile([P, H], U8, name="w1_plane%d" % a, align_bytes=64)
+            nc.vector.quantize_mx(
+                out=codes[:].bitcast(FP8X4), scales=plane[:], in_=w1_bf[a][:].rearrange("p c i -> p (c i)")
+            )
+            w1_codes.append(codes)
+            w1_plane.append(plane)
+
+        def bound_lower(jt):
+            t_low = keep.tile(
+                [P, 4, P], F32, name="low%d" % jt, tag="w1_bf0" if jt == 0 else "low%d" % jt, align_bytes=64
+            )
+            sums = banks[jt][:].rearrange("p (q t) -> p t q", t=4)
+            if jt % 2 == 0:
+                nc.vector.tensor_scalar(
+                    out=t_low[:], in0=sums, scalar1=cols[:, jt : jt + 1], scalar2=cols[:, jt : jt + 1],
+                    op0=ALU.min, op1=ALU.add,
+                )
+            else:
+                short = shared.tile([P, 4, P], F32, name="short%d" % jt, offset=(jt // 2) * 4 * H)
+                nc.scalar.activation(short[:], sums, ACT.Relu, bias=cols[:, jt : jt + 1], scale=-1.0)
+                nc.gpsimd.tensor_scalar(
+                    out=t_low[:].rearrange("p t q -> p (t q)"), in0=short[:].rearrange("p t q -> p (t q)"),
+                    scalar1=-1.0, scalar2=twice_level[:, jt : jt + 1], op0=ALU.mult, op1=ALU.add,
+                )
+            low.append(t_low)
+
+        def upper_pass(a, jt):
+            words, scales = v_operand(a, jt)
+            nc.tensor.matmul_mx(
+                out=banks[jt][:], lhsT=words, lhsT_scale=scales,
+                rhs=w1_codes[a][:].bitcast(FP8X4), rhs_scale=w1_plane[a][:],
+                start=(a == 0), stop=(a == PASSES - 1),
+            )
+
+        for a in range(PASSES):
+            round_w1(a)
+        quantise_w1(0)
+        for jt in range(JT // 2):
+            bound_lower(jt)
+        quantise_w1(1)
+        for jt in range(JT // 2, JT):
+            bound_lower(jt)
+        quantise_w1(2)
+        for a in range(PASSES):
+            for jt in range(JT):
+                upper_pass(a, jt)
+
+        v2_sc = [
+            shared.tile([P, HALF], U8, name="v2_sc0", offset=12 * T, align_bytes=64),
+            keep.tile([P, HALF], U8, name="v2_sc1", tag="w1_bf1", align_bytes=64),
+        ]
+        for h in range(2):
+            nc.vector.tensor_copy(v2_sc[h][:], tab2_sc[:].indirect(offs2_sb[:, 32 * h : 32 * (h + 1)]))
+        v2_w = keep.tile([P, S2], U32, name="v2_w", tag="w1_bf%d" % (PASSES - 1), align_bytes=64)
 
         def gather_v2(i):
-            nc.vector.tensor_copy(v2_w[i][:], tab2_w[:].indirect(offs2_sb[:, 16 * i : 16 * (i + 1)]))
+            nc.vector.tensor_copy(v2_w[:, 256 * i : 256 * (i + 1)], tab2_w[:].indirect(offs2_sb[:, 16 * i : 16 * (i + 1)]))
 
         gather_v2(0)
 
@@ -205,8 +283,8 @@ def tile_list_ripening_schedule_scores_kernel(
             for h in range(2):
                 bank = banks[(2 * m + h) % 8]
                 nc.tensor.matmul_mx(
-                    out=bank[:], lhsT=v2_w[m // 2][:, (m % 2) * P : (m % 2 + 1) * P].bitcast(FP8X4),
-                    lhsT_scale=v2_sc[:, m * P : (m + 1) * P],
+                    out=bank[:], lhsT=v2_w[:, m * P : (m + 1) * P].bitcast(FP8X4),
+                    lhsT_scale=v2_sc[m // 4][:, (m % 4) * P : (m % 4 + 1) * P],
                     rhs=h_codes[h][:].bitcast(FP8X4), rhs_scale=h_plane[h][:], start=True, stop=True,
                 )
                 nc.scalar.copy(e[:, h * HALF : (h + 1) * HALF], bank[:])

@@ -22,7 +22,8 @@ PASSES = K // 512
 JT = S // P
 MT = S2 // P
 HALF = 512
-SCALAR_COLUMNS = (256, 128, 256)
+KB = 1024
+RAW_AT = (0, 10 * KB)
 
 
 def tile_list_ripening_schedule_scores_kernel(
@@ -42,7 +43,7 @@ def tile_list_ripening_schedule_scores_kernel(
         pos1_sb = keep.tile([P, NP // 16], U16, name="pos1_sb")
         pos2_sb = keep.tile([P, NP // 16], U16, name="pos2_sb")
 
-        tab_sc = keep.tile([P, T], U8, name="tab_sc", tag="tab_sc", align_bytes=64)
+        tab_sc = shared.tile([P, T], U8, name="tab_sc", offset=7 * KB, align_bytes=64)
         tab2_sc = keep.tile([P, T3], U8, name="tab2_sc", align_bytes=64)
         w4_sc = keep.tile([P, PASSES, H], U8, name="w4_sc", align_bytes=64)
         w4_w = keep.tile([P, PASSES, 2 * H], U8, name="w4_w", align_bytes=64)
@@ -69,9 +70,9 @@ def tile_list_ripening_schedule_scores_kernel(
             )
 
         tab_w = [
-            shared.tile([P, T], U32, name="tab_w0", offset=2 * T),
+            shared.tile([P, T], U32, name="tab_w0", offset=RAW_AT[1]),
             keep.tile([P, T], U32, name="tab_w1", tag="stage1", align_bytes=64),
-            shared.tile([P, T], U32, name="tab_w2", offset=8 * T + HALF),
+            shared.tile([P, T], U32, name="tab_w2", offset=18 * KB + HALF),
         ]
         nc.sync.dma_start(offs_sb[:], offs)
         nc.sync.dma_start(offs2_sb[:], offs2)
@@ -100,46 +101,48 @@ def tile_list_ripening_schedule_scores_kernel(
             )
         nc.gpsimd.dma_start(out=gain_sb[:], in_=gain.rearrange("(p t) -> p t", t=4))
 
-        v_w = [
-            [
-                keep.tile(
-                    [P, HALF], U32, name="v_w%d_%d" % (a, h),
-                    tag="tab_sc" if (a, h) == (0, 1) else "v_w%d_%d" % (a, h), align_bytes=64,
-                )
-                for h in range(2)
-            ]
-            for a in range(PASSES)
-        ]
+        v_w = {}
+        for a in range(PASSES):
+            for h in range(2):
+                if (a, h) == (0, 1):
+                    v_w[a, h] = shared.tile([P, HALF], U32, name="v_w01", offset=8 * KB, align_bytes=64)
+                else:
+                    v_w[a, h] = keep.tile([P, HALF], U32, name="v_w%d%d" % (a, h), align_bytes=64)
 
         def gather_v(a, h):
-            nc.vector.tensor_copy(v_w[a][h][:], tab_w[a][:].indirect(offs_sb[:, 32 * h : 32 * (h + 1)]))
+            nc.vector.tensor_copy(v_w[a, h][:], tab_w[a][:].indirect(offs_sb[:, 32 * h : 32 * (h + 1)]))
 
         gather_v(0, 0)
         for h in range(2):
             nc.vector.tensor_copy(
                 v_sc[0][:, h * HALF : (h + 1) * HALF], tab_sc[:].indirect(offs_sb[:, 32 * h : 32 * (h + 1)])
             )
-        for a in range(1, PASSES):
-            nc.sync.dma_start(out=v_sc[a][0:112, :].bitcast(I32), in_=v_sc[0][4 * a : 4 * a + 112, :].bitcast(I32))
-
         w1_raw = [
-            shared.tile([P, 4, H], F32, name="w1_raw0", offset=0),
-            shared.tile([P, 4, H], F32, name="w1_raw1", offset=4 * T),
+            shared.tile([P, 4, H], F32, name="w1_raw0", offset=RAW_AT[0]),
+            shared.tile([P, 4, H], F32, name="w1_raw1", offset=RAW_AT[1]),
             keep.tile([P, 4, H], F32, name="w1_raw2", tag="stage1", align_bytes=64),
         ]
-        tab2_w = shared.tile([P, T3], U32, name="tab2_w", offset=8 * T)
+
+        def load_w1(a):
+            nc.sync.dma_start(
+                out=w1_raw[a][:], in_=w1[512 * a : 512 * (a + 1), :].rearrange("(p i) c -> p i c", i=4)
+            )
+
+        for a in range(1, PASSES):
+            nc.sync.dma_start(out=v_sc[a][0:112, :].bitcast(I32), in_=v_sc[0][4 * a : 4 * a + 112, :].bitcast(I32))
+            if a == 1:
+                load_w1(0)
+        tab2_w = shared.tile([P, T3], U32, name="tab2_w", offset=18 * KB)
 
         nc.tensor.transpose(banks[7][:, 0:P], rows[:], ident[:])
         cols = keep.tile([P, JT + MT], F32, name="cols")
         neg_level = keep.tile([P, JT], F32, name="neg_level")
         nc.scalar.copy(cols[:], banks[7][:, 0 : JT + MT])
         nc.scalar.activation(neg_level[:], banks[7][:, 0:JT], ACT.Copy, scale=-1.0)
-        twice_level = keep.tile([P, JT], F32, name="twice_level")
-        nc.scalar.activation(twice_level[:], banks[7][:, 0:JT], ACT.Copy, scale=2.0)
 
         def v_operand(a, jt):
             h, c = divmod(jt * P, HALF)
-            return v_w[a][h][:, c : c + P].bitcast(FP8X4), v_sc[a][:, jt * P : (jt + 1) * P]
+            return v_w[a, h][:, c : c + P].bitcast(FP8X4), v_sc[a][:, jt * P : (jt + 1) * P]
 
         for a in range(PASSES):
             for h in range(2):
@@ -153,10 +156,8 @@ def tile_list_ripening_schedule_scores_kernel(
                     start=(a == 0), stop=(a == PASSES - 1),
                 )
 
-        for a in range(PASSES):
-            nc.sync.dma_start(
-                out=w1_raw[a][:], in_=w1[512 * a : 512 * (a + 1), :].rearrange("(p i) c -> p i c", i=4)
-            )
+        load_w1(1)
+        load_w1(2)
         load_words(tab2_w, tab2_words[0])
 
         w1_bf, w1_codes, w1_plane, low = [], [], [], []
@@ -170,13 +171,7 @@ def tile_list_ripening_schedule_scores_kernel(
                     w1_raw[a][:, :, c0:c1].rearrange("p i (c n) -> p c i n", n=4),
                 )
 
-            split = SCALAR_COLUMNS[a]
-            nc.scalar.copy(*by_fours(0, split))
-            for c in range(split, H, P):
-                nc.gpsimd.tensor_scalar(
-                    out=grouped[:, c : c + P, :], in0=w1_raw[a][:, :, c : c + P].rearrange("p i c -> p c i"),
-                    scalar1=1.0, scalar2=0.0, op0=ALU.mult, op1=ALU.add,
-                )
+            nc.scalar.copy(*by_fours(0, H))
             w1_bf.append(grouped)
 
         def quantise_w1(a):
@@ -189,22 +184,15 @@ def tile_list_ripening_schedule_scores_kernel(
             w1_plane.append(plane)
 
         def bound_lower(jt):
-            t_low = keep.tile(
-                [P, 4, P], F32, name="low%d" % jt, tag="w1_bf0" if jt == 0 else "low%d" % jt, align_bytes=64
-            )
-            sums = banks[jt][:].rearrange("p (q t) -> p t q", t=4)
-            if jt % 2 == 0:
-                nc.vector.tensor_scalar(
-                    out=t_low[:], in0=sums, scalar1=cols[:, jt : jt + 1], scalar2=cols[:, jt : jt + 1],
-                    op0=ALU.min, op1=ALU.add,
-                )
+            if jt < 2:
+                t_low = keep.tile([P, 4, P], F32, name="low%d" % jt)
             else:
-                short = shared.tile([P, 4, P], F32, name="short%d" % jt, offset=(jt // 2) * 4 * H)
-                nc.scalar.activation(short[:], sums, ACT.Relu, bias=cols[:, jt : jt + 1], scale=-1.0)
-                nc.gpsimd.tensor_scalar(
-                    out=t_low[:].rearrange("p t q -> p (t q)"), in0=short[:].rearrange("p t q -> p (t q)"),
-                    scalar1=-1.0, scalar2=twice_level[:, jt : jt + 1], op0=ALU.mult, op1=ALU.add,
-                )
+                a, slot = divmod(jt - 2, 3)
+                t_low = shared.tile([P, 4, P], F32, name="low%d" % jt, offset=RAW_AT[a] + slot * 4 * H)
+            nc.vector.tensor_scalar(
+                out=t_low[:], in0=banks[jt][:].rearrange("p (q t) -> p t q", t=4),
+                scalar1=cols[:, jt : jt + 1], scalar2=cols[:, jt : jt + 1], op0=ALU.min, op1=ALU.add,
+            )
             low.append(t_low)
 
         def upper_pass(a, jt):
@@ -217,20 +205,17 @@ def tile_list_ripening_schedule_scores_kernel(
 
         for a in range(PASSES):
             round_w1(a)
-        quantise_w1(0)
-        for jt in range(JT // 2):
-            bound_lower(jt)
-        quantise_w1(1)
-        for jt in range(JT // 2, JT):
-            bound_lower(jt)
-        quantise_w1(2)
+        for a, tiles in enumerate((range(0, 2), range(2, 5), range(5, JT))):
+            for jt in tiles:
+                bound_lower(jt)
+            quantise_w1(a)
         for a in range(PASSES):
             for jt in range(JT):
                 upper_pass(a, jt)
 
         v2_sc = [
-            shared.tile([P, HALF], U8, name="v2_sc0", offset=12 * T, align_bytes=64),
-            keep.tile([P, HALF], U8, name="v2_sc1", tag="w1_bf1", align_bytes=64),
+            shared.tile([P, HALF], U8, name="v2_sc0", offset=26 * KB, align_bytes=64),
+            keep.tile([P, HALF], U8, name="v2_sc1", tag="stage1", align_bytes=64),
         ]
         for h in range(2):
             nc.vector.tensor_copy(v2_sc[h][:], tab2_sc[:].indirect(offs2_sb[:, 32 * h : 32 * (h + 1)]))
@@ -277,17 +262,24 @@ def tile_list_ripening_schedule_scores_kernel(
 
         scores = {}
         arrival = {}
+        used = []
 
         def make_scores(m):
             e = ring.tile([P, S], F32, name="e", bufs=4)
-            for h in range(2):
-                bank = banks[(2 * m + h) % 8]
+            widths = (512, 256, 128, 128) if m == 0 else (512, 512)
+            start = 0
+            for width in widths:
+                h, c = divmod(start, HALF)
+                bank = banks[len(used) % 8]
+                used.append(bank)
                 nc.tensor.matmul_mx(
-                    out=bank[:], lhsT=v2_w[:, m * P : (m + 1) * P].bitcast(FP8X4),
+                    out=bank[:, 0:width], lhsT=v2_w[:, m * P : (m + 1) * P].bitcast(FP8X4),
                     lhsT_scale=v2_sc[m // 4][:, (m % 4) * P : (m % 4 + 1) * P],
-                    rhs=h_codes[h][:].bitcast(FP8X4), rhs_scale=h_plane[h][:], start=True, stop=True,
+                    rhs=h_codes[h][:, c : c + width].bitcast(FP8X4), rhs_scale=h_plane[h][:, c : c + width],
+                    start=True, stop=True,
                 )
-                nc.scalar.copy(e[:, h * HALF : (h + 1) * HALF], bank[:])
+                nc.scalar.copy(e[:, start : start + width], bank[:, 0:width])
+                start += width
             scores[m] = e
 
         def pick_first(m):
@@ -299,8 +291,13 @@ def tile_list_ripening_schedule_scores_kernel(
 
         def pick_second(m):
             res = ring.tile([P, NP], F32, name="res")
-            nc.vector.tensor_tensor(res[:], scores[m][:].indirect(pos2_sb[:]), arrival[m][:], ALU.mult)
-            nc.sync.dma_start(out=out[m * P : (m + 1) * P, :], in_=res[:])
+            width = NP // 2 if m == MT - 1 else NP
+            for c in range(0, NP, width):
+                nc.vector.tensor_tensor(
+                    res[:, c : c + width], scores[m][:].indirect(pos2_sb[:, c // 16 : (c + width) // 16]),
+                    arrival[m][:, c : c + width], ALU.mult,
+                )
+                nc.sync.dma_start(out=out[m * P : (m + 1) * P, c : c + width], in_=res[:, c : c + width])
 
         make_scores(0)
         make_scores(1)

@@ -23,6 +23,8 @@ JT = S // P
 MT = S2 // P
 HALF = 512
 KB = 1024
+VECTOR_SUMS = 2
+SCALAR_GAIN_TILES = (2, 4)
 RAW_AT = (0, 10 * KB)
 
 
@@ -189,10 +191,12 @@ def tile_list_ripening_schedule_scores_kernel(
             else:
                 a, slot = divmod(jt - 2, 3)
                 t_low = shared.tile([P, 4, P], F32, name="low%d" % jt, offset=RAW_AT[a] + slot * 4 * H)
-            nc.vector.tensor_scalar(
-                out=t_low[:], in0=banks[jt][:].rearrange("p (q t) -> p t q", t=4),
-                scalar1=cols[:, jt : jt + 1], scalar2=cols[:, jt : jt + 1], op0=ALU.min, op1=ALU.add,
-            )
+            sums = banks[jt][:].rearrange("p (q t) -> p t q", t=4)
+            lev = cols[:, jt : jt + 1]
+            if jt < VECTOR_SUMS:
+                nc.vector.tensor_scalar(out=t_low[:], in0=sums, scalar1=lev, scalar2=None, op0=ALU.min)
+            else:
+                nc.vector.tensor_scalar(out=t_low[:], in0=sums, scalar1=lev, scalar2=lev, op0=ALU.min, op1=ALU.add)
             low.append(t_low)
 
         def upper_pass(a, jt):
@@ -219,10 +223,11 @@ def tile_list_ripening_schedule_scores_kernel(
         ]
         for h in range(2):
             nc.vector.tensor_copy(v2_sc[h][:], tab2_sc[:].indirect(offs2_sb[:, 32 * h : 32 * (h + 1)]))
-        v2_w = keep.tile([P, S2], U32, name="v2_w", tag="w1_bf%d" % (PASSES - 1), align_bytes=64)
+        v2_first = keep.tile([P, 2 * P], U32, name="v2_first", tag="w1_bf%d" % (PASSES - 1), align_bytes=64)
+        v2_w = [v2_first[:]]
 
         def gather_v2(i):
-            nc.vector.tensor_copy(v2_w[:, 256 * i : 256 * (i + 1)], tab2_w[:].indirect(offs2_sb[:, 16 * i : 16 * (i + 1)]))
+            nc.vector.tensor_copy(v2_w[i], tab2_w[:].indirect(offs2_sb[:, 16 * i : 16 * (i + 1)]))
 
         gather_v2(0)
 
@@ -240,25 +245,45 @@ def tile_list_ripening_schedule_scores_kernel(
         ups = []
         for jt in range(JT):
             up = keep.tile([P, 4, P], F32, name="up%d" % jt)
-            nc.scalar.activation(
-                up[:], banks[jt][:].rearrange("p (q t) -> p t q", t=4), ACT.Relu,
-                bias=neg_level[:, jt : jt + 1], scale=1.0,
-            )
+            sums = banks[jt][:].rearrange("p (q t) -> p t q", t=4)
+            if jt < VECTOR_SUMS:
+                nc.vector.scalar_tensor_tensor(
+                    out=up[:], in0=sums, scalar=cols[:, jt : jt + 1], in1=low[jt][:], op0=ALU.max, op1=ALU.add
+                )
+            else:
+                nc.scalar.activation(up[:], sums, ACT.Relu, bias=neg_level[:, jt : jt + 1], scale=1.0)
             ups.append(up)
         for jt in range(JT):
             for t in range(4):
                 dst = banks[jt][:, t * P : (t + 1) * P]
-                nc.tensor.matmul(dst, lhsT=low[jt][:, t, :], rhs=ident[:], start=True, stop=False, is_transpose=True)
-                nc.tensor.matmul(dst, lhsT=ups[jt][:, t, :], rhs=ident[:], start=False, stop=True, is_transpose=True)
-            hb = keep.tile([P, P, 4], BF16, name="h_bf%d" % jt, align_bytes=64)
-            nc.vector.tensor_tensor(
-                out=hb[:], in0=banks[jt][:].rearrange("p (t j) -> p j t", t=4),
-                in1=gain_sb[:].unsqueeze(1).to_broadcast([P, P, 4]), op=ALU.mult,
-            )
+                terms = (ups[jt],) if jt < VECTOR_SUMS else (low[jt], ups[jt])
+                for n, term in enumerate(terms):
+                    nc.tensor.matmul(
+                        dst, lhsT=term[:, t, :], rhs=ident[:],
+                        start=(n == 0), stop=(n == len(terms) - 1), is_transpose=True,
+                    )
+            hb = keep.tile([P, P, 4], BF16, name="h_bf%d" % jt, tag="h_bf%d" % jt, align_bytes=64)
+            if jt in SCALAR_GAIN_TILES:
+                by_rows = ring.tile([P, 4, P], BF16, name="by_rows")
+                for t in range(4):
+                    nc.scalar.activation(
+                        by_rows[:, t, :], banks[jt][:, t * P : (t + 1) * P], ACT.Copy, scale=gain_sb[:, t : t + 1]
+                    )
+                nc.scalar.copy(
+                    hb[:].rearrange("p (c n) t -> p c t n", n=4), by_rows[:].rearrange("p t (c n) -> p c t n", n=4)
+                )
+            else:
+                nc.vector.tensor_tensor(
+                    out=hb[:], in0=banks[jt][:].rearrange("p (t j) -> p j t", t=4),
+                    in1=gain_sb[:].unsqueeze(1).to_broadcast([P, P, 4]), op=ALU.mult,
+                )
             h_bf.append(hb)
             if jt > 0:
                 quantise_h(jt - 1)
         quantise_h(JT - 1)
+
+        v2_rest = keep.tile([P, S2 - 2 * P], U32, name="v2_rest", tag="h_bf%d" % (JT - 1), align_bytes=64)
+        v2_w.extend(v2_rest[:, c : c + 2 * P] for c in range(0, S2 - 2 * P, 2 * P))
 
         scores = {}
         arrival = {}
@@ -273,7 +298,7 @@ def tile_list_ripening_schedule_scores_kernel(
                 bank = banks[len(used) % 8]
                 used.append(bank)
                 nc.tensor.matmul_mx(
-                    out=bank[:, 0:width], lhsT=v2_w[:, m * P : (m + 1) * P].bitcast(FP8X4),
+                    out=bank[:, 0:width], lhsT=v2_w[m // 2][:, (m % 2) * P : (m % 2 + 1) * P].bitcast(FP8X4),
                     lhsT_scale=v2_sc[m // 4][:, (m % 4) * P : (m % 4 + 1) * P],
                     rhs=h_codes[h][:, c : c + width].bitcast(FP8X4), rhs_scale=h_plane[h][:, c : c + width],
                     start=True, stop=True,

from contextlib import ExitStack

import concourse.mybir as mybir
from concourse.masks import make_identity

K, H, T, S, S2, T3, NP = 1536, 512, 2048, 1024, 1024, 2048, 512
FLOPS = 2 * (2 * K * H * S + H * S2 * S)

F32 = mybir.dt.float32
BF16 = mybir.dt.bfloat16
I32 = mybir.dt.int32
U32 = mybir.dt.uint32
U16 = mybir.dt.uint16
U8 = mybir.dt.uint8
FP8X4 = mybir.dt.float8_e4m3fn_x4
FP4X4 = mybir.dt.float4_e2m1fn_x4
ALU = mybir.AluOpType
ACT = mybir.ActivationFunctionType

P = 128
PASSES = K // 512
JT = S // P
MT = S2 // P
HALF = 512
KB = 1024
VECTOR_SUMS = 2
SCALAR_GAIN_TILES = (2, 4)
RAW_AT = (0, 10 * KB)


def tile_list_ripening_schedule_scores_kernel(
    tc, tab_words, tab_scales, offs, w1, w4_words, w4_scales, level, gain,
    tab2_words, tab2_scales, offs2, shift, pos1, pos2, out,
):
    nc = tc.nc
    with ExitStack() as ctx:
        keep = ctx.enter_context(tc.tile_pool(name="keep", bufs=1))
        ring = ctx.enter_context(tc.tile_pool(name="ring", bufs=3))
        shared = ctx.enter_context(tc.tile_pool(name="shared", bufs=1))
        psum = ctx.enter_context(tc.psum_pool(name="psum", bufs=1))
        banks = [psum.tile([P, 512], F32, name="bank%d" % b) for b in range(8)]

        offs_sb = keep.tile([P, S // 16], U16, name="offs_sb")
        offs2_sb = keep.tile([P, S2 // 16], U16, name="offs2_sb")
        pos1_sb = keep.tile([P, NP // 16], U16, name="pos1_sb")
        pos2_sb = keep.tile([P, NP // 16], U16, name="pos2_sb")

        tab_sc = shared.tile([P, T], U8, name="tab_sc", offset=7 * KB, align_bytes=64)
        tab2_sc = keep.tile([P, T3], U8, name="tab2_sc", align_bytes=64)
        w4_sc = keep.tile([P, PASSES, H], U8, name="w4_sc", align_bytes=64)
        w4_w = keep.tile([P, PASSES, 2 * H], U8, name="w4_w", align_bytes=64)
        v_sc = [keep.tile([P, S], U8, name="v_sc%d" % a, align_bytes=64) for a in range(PASSES)]
        rows = keep.tile([P, P], F32, name="rows")
        ident = keep.tile([P, P], F32, name="ident")
        gain_sb = keep.tile([P, 4], F32, name="gain_sb")

        nc.gpsimd.memset(tab_sc[:, 0 : T // 2].bitcast(I32), 0)
        nc.vector.memset(tab_sc[:, T // 2 : T].bitcast(I32), 0)
        nc.gpsimd.memset(rows[:], 0.0)
        nc.vector.memset(w4_sc[:].rearrange("p a n -> p (a n)").bitcast(I32), 0)
        for a in range(1, PASSES):
            nc.vector.memset(v_sc[a][96:128, :].bitcast(I32), 0)
        nc.vector.memset(tab2_sc[:].bitcast(I32), 0)

        def load_words(win, words):
            nc.sync.dma_start(out=win[:].bitcast(I32), in_=words.rearrange("p t i -> p (t i)").bitcast(I32))

        def load_w4_scales(q):
            nc.sync.dma_start(
                out=w4_sc[32 * q : 32 * q + 4, :, :].bitcast(I32),
                in_=w4_scales[:, 4 * q : 4 * q + 4, :].rearrange("a r n -> r a n").bitcast(I32),
            )

        tab_w = [
            shared.tile([P, T], U32, name="tab_w0", offset=RAW_AT[1]),
            keep.tile([P, T], U32, name="tab_w1", tag="stage1", align_bytes=64),
            shared.tile([P, T], U32, name="tab_w2", offset=18 * KB + HALF),
        ]
        nc.sync.dma_start(offs_sb[:], offs)
        nc.sync.dma_start(offs2_sb[:], offs2)
        nc.sync.dma_start(pos1_sb[:], pos1)
        load_words(tab_w[0], tab_words[0])
        for q, queue in enumerate((nc.scalar, nc.sync, nc.scalar, nc.sync)):
            queue.dma_start(
                out=tab_sc[32 * q : 32 * q + 4 * PASSES, :].bitcast(I32),
                in_=tab_scales[:, 4 * q : 4 * q + 4, :].bitcast(I32),
            )
        load_w4_scales(0)
        load_w4_scales(1)
        nc.sync.dma_start(out=w4_w[:].bitcast(I32), in_=w4_words.rearrange("a p n -> p a n").bitcast(I32))
        load_w4_scales(2)
        load_w4_scales(3)
        load_words(tab_w[1], tab_words[1])
        load_words(tab_w[2], tab_words[2])
        nc.sync.dma_start(pos2_sb[:], pos2)
        nc.gpsimd.dma_start(out=rows[0:JT, :], in_=level.rearrange("(t p) -> t p", p=P))
        nc.gpsimd.dma_start(out=rows[JT : JT + MT, :], in_=shift.rearrange("(t p) -> t p", p=P))
        make_identity(nc, ident[:])
        for q in range(4):
            nc.gpsimd.dma_start(
                out=tab2_sc[32 * q : 32 * q + 4, :].bitcast(I32),
                in_=tab2_scales[0, 4 * q : 4 * q + 4, :].bitcast(I32),
            )
        nc.gpsimd.dma_start(out=gain_sb[:], in_=gain.rearrange("(p t) -> p t", t=4))

        v_w = {}
        for a in range(PASSES):
            for h in range(2):
                if (a, h) == (0, 1):
                    v_w[a, h] = shared.tile([P, HALF], U32, name="v_w01", offset=8 * KB, align_bytes=64)
                else:
                    v_w[a, h] = keep.tile([P, HALF], U32, name="v_w%d%d" % (a, h), align_bytes=64)

        def gather_v(a, h):
            nc.vector.tensor_copy(v_w[a, h][:], tab_w[a][:].indirect(offs_sb[:, 32 * h : 32 * (h + 1)]))

        gather_v(0, 0)
        for h in range(2):
            nc.vector.tensor_copy(
                v_sc[0][:, h * HALF : (h + 1) * HALF], tab_sc[:].indirect(offs_sb[:, 32 * h : 32 * (h + 1)])
            )
        w1_raw = [
            shared.tile([P, 4, H], F32, name="w1_raw0", offset=RAW_AT[0]),
            shared.tile([P, 4, H], F32, name="w1_raw1", offset=RAW_AT[1]),
            keep.tile([P, 4, H], F32, name="w1_raw2", tag="stage1", align_bytes=64),
        ]

        def load_w1(a):
            nc.sync.dma_start(
                out=w1_raw[a][:], in_=w1[512 * a : 512 * (a + 1), :].rearrange("(p i) c -> p i c", i=4)
            )

        for a in range(1, PASSES):
            nc.sync.dma_start(out=v_sc[a][0:112, :].bitcast(I32), in_=v_sc[0][4 * a : 4 * a + 112, :].bitcast(I32))
            if a == 1:
                load_w1(0)
        tab2_w = shared.tile([P, T3], U32, name="tab2_w", offset=18 * KB)

        nc.tensor.transpose(banks[7][:, 0:P], rows[:], ident[:])
        cols = keep.tile([P, JT + MT], F32, name="cols")
        neg_level = keep.tile([P, JT], F32, name="neg_level")
        nc.scalar.copy(cols[:], banks[7][:, 0 : JT + MT])
        nc.scalar.activation(neg_level[:], banks[7][:, 0:JT], ACT.Copy, scale=-1.0)

        def v_operand(a, jt):
            h, c = divmod(jt * P, HALF)
            return v_w[a, h][:, c : c + P].bitcast(FP8X4), v_sc[a][:, jt * P : (jt + 1) * P]

        for a in range(PASSES):
            for h in range(2):
                if (a, h) != (0, 0):
                    gather_v(a, h)
            for jt in range(JT):
                words, scales = v_operand(a, jt)
                nc.tensor.matmul_mx(
                    out=banks[jt][:], lhsT=words, lhsT_scale=scales,
                    rhs=w4_w[:, a, :].bitcast(FP4X4), rhs_scale=w4_sc[:, a, :],
                    start=(a == 0), stop=(a == PASSES - 1),
                )

        load_w1(1)
        load_w1(2)
        load_words(tab2_w, tab2_words[0])

        w1_bf, w1_codes, w1_plane, low = [], [], [], []

        def round_w1(a):
            grouped = keep.tile([P, H, 4], BF16, name="w1_bf%d" % a, tag="w1_bf%d" % a, align_bytes=64)

            def by_fours(c0, c1):
                return (
                    grouped[:, c0:c1, :].rearrange("p (c n) i -> p c i n", n=4),
                    w1_raw[a][:, :, c0:c1].rearrange("p i (c n) -> p c i n", n=4),
                )

            nc.scalar.copy(*by_fours(0, H))
            w1_bf.append(grouped)

        def quantise_w1(a):
            codes = keep.tile([P, H], U32, name="w1_codes%d" % a, align_bytes=64)
            plane = keep.tile([P, H], U8, name="w1_plane%d" % a, align_bytes=64)
            nc.vector.quantize_mx(
                out=codes[:].bitcast(FP8X4), scales=plane[:], in_=w1_bf[a][:].rearrange("p c i -> p (c i)")
            )
            w1_codes.append(codes)
            w1_plane.append(plane)

        def bound_lower(jt):
            if jt < 2:
                t_low = keep.tile([P, 4, P], F32, name="low%d" % jt)
            else:
                a, slot = divmod(jt - 2, 3)
                t_low = shared.tile([P, 4, P], F32, name="low%d" % jt, offset=RAW_AT[a] + slot * 4 * H)
            sums = banks[jt][:].rearrange("p (q t) -> p t q", t=4)
            lev = cols[:, jt : jt + 1]
            if jt < VECTOR_SUMS:
                nc.vector.tensor_scalar(out=t_low[:], in0=sums, scalar1=lev, scalar2=None, op0=ALU.min)
            else:
                nc.vector.tensor_scalar(out=t_low[:], in0=sums, scalar1=lev, scalar2=lev, op0=ALU.min, op1=ALU.add)
            low.append(t_low)

        def upper_pass(a, jt):
            words, scales = v_operand(a, jt)
            nc.tensor.matmul_mx(
                out=banks[jt][:], lhsT=words, lhsT_scale=scales,
                rhs=w1_codes[a][:].bitcast(FP8X4), rhs_scale=w1_plane[a][:],
                start=(a == 0), stop=(a == PASSES - 1),
            )

        for a in range(PASSES):
            round_w1(a)
        for a, tiles in enumerate((range(0, 2), range(2, 5), range(5, JT))):
            for jt in tiles:
                bound_lower(jt)
            quantise_w1(a)
        for a in range(PASSES):
            for jt in range(JT):
                upper_pass(a, jt)

        v2_sc = [
            shared.tile([P, HALF], U8, name="v2_sc0", offset=26 * KB, align_bytes=64),
            keep.tile([P, HALF], U8, name="v2_sc1", tag="stage1", align_bytes=64),
        ]
        for h in range(2):
            nc.vector.tensor_copy(v2_sc[h][:], tab2_sc[:].indirect(offs2_sb[:, 32 * h : 32 * (h + 1)]))
        v2_first = keep.tile([P, 2 * P], U32, name="v2_first", tag="w1_bf%d" % (PASSES - 1), align_bytes=64)
        v2_w = [v2_first[:]]

        def gather_v2(i):
            nc.vector.tensor_copy(v2_w[i], tab2_w[:].indirect(offs2_sb[:, 16 * i : 16 * (i + 1)]))

        gather_v2(0)

        h_codes = [keep.tile([P, HALF], U32, name="h_codes%d" % h, align_bytes=64) for h in range(2)]
        h_plane = [keep.tile([P, HALF], U8, name="h_plane%d" % h, align_bytes=64) for h in range(2)]
        h_bf = []

        def quantise_h(jt):
            h, c = divmod(jt * P, HALF)
            nc.vector.quantize_mx(
                out=h_codes[h][:, c : c + P].bitcast(FP8X4), scales=h_plane[h][:, c : c + P],
                in_=h_bf[jt][:].rearrange("p j t -> p (j t)"),
            )

        ups = []
        for jt in range(JT):
            up = keep.tile([P, 4, P], F32, name="up%d" % jt)
            sums = banks[jt][:].rearrange("p (q t) -> p t q", t=4)
            if jt < VECTOR_SUMS:
                nc.vector.scalar_tensor_tensor(
                    out=up[:], in0=sums, scalar=cols[:, jt : jt + 1], in1=low[jt][:], op0=ALU.max, op1=ALU.add
                )
            else:
                nc.scalar.activation(up[:], sums, ACT.Relu, bias=neg_level[:, jt : jt + 1], scale=1.0)
            ups.append(up)
        for jt in range(JT):
            for t in range(4):
                dst = banks[jt][:, t * P : (t + 1) * P]
                terms = (ups[jt],) if jt < VECTOR_SUMS else (low[jt], ups[jt])
                for n, term in enumerate(terms):
                    nc.tensor.matmul(
                        dst, lhsT=term[:, t, :], rhs=ident[:],
                        start=(n == 0), stop=(n == len(terms) - 1), is_transpose=True,
                    )
            hb = keep.tile([P, P, 4], BF16, name="h_bf%d" % jt, tag="h_bf%d" % jt, align_bytes=64)
            if jt in SCALAR_GAIN_TILES:
                by_rows = ring.tile([P, 4, P], BF16, name="by_rows")
                for t in range(4):
                    nc.scalar.activation(
                        by_rows[:, t, :], banks[jt][:, t * P : (t + 1) * P], ACT.Copy, scale=gain_sb[:, t : t + 1]
                    )
                nc.scalar.copy(
                    hb[:].rearrange("p (c n) t -> p c t n", n=4), by_rows[:].rearrange("p t (c n) -> p c t n", n=4)
                )
            else:
                nc.vector.tensor_tensor(
                    out=hb[:], in0=banks[jt][:].rearrange("p (t j) -> p j t", t=4),
                    in1=gain_sb[:].unsqueeze(1).to_broadcast([P, P, 4]), op=ALU.mult,
                )
            h_bf.append(hb)
            if jt > 0:
                quantise_h(jt - 1)
        quantise_h(JT - 1)

        v2_rest = keep.tile([P, S2 - 2 * P], U32, name="v2_rest", tag="h_bf%d" % (JT - 1), align_bytes=64)
        v2_w.extend(v2_rest[:, c : c + 2 * P] for c in range(0, S2 - 2 * P, 2 * P))

        scores = {}
        arrival = {}
        used = []

        def make_scores(m):
            e = ring.tile([P, S], F32, name="e", bufs=4)
            widths = (512, 256, 128, 128) if m == 0 else (512, 512)
            start = 0
            for width in widths:
                h, c = divmod(start, HALF)
                bank = banks[len(used) % 8]
                used.append(bank)
                nc.tensor.matmul_mx(
                    out=bank[:, 0:width], lhsT=v2_w[m // 2][:, (m % 2) * P : (m % 2 + 1) * P].bitcast(FP8X4),
                    lhsT_scale=v2_sc[m // 4][:, (m % 4) * P : (m % 4 + 1) * P],
                    rhs=h_codes[h][:, c : c + width].bitcast(FP8X4), rhs_scale=h_plane[h][:, c : c + width],
                    start=True, stop=True,
                )
                nc.scalar.copy(e[:, start : start + width], bank[:, 0:width])
                start += width
            scores[m] = e

        def pick_first(m):
            picked = ring.tile([P, NP], F32, name="picked")
            nc.vector.tensor_copy(picked[:], scores[m][:].indirect(pos1_sb[:]))
            arr = ring.tile([P, NP], F32, name="arr")
            nc.scalar.activation(arr[:], picked[:], ACT.Abs, bias=cols[:, JT + m : JT + m + 1], scale=1.0)
            arrival[m] = arr

        def pick_second(m):
            res = ring.tile([P, NP], F32, name="res")
            width = NP // 2 if m == MT - 1 else NP
            for c in range(0, NP, width):
                nc.vector.tensor_tensor(
                    res[:, c : c + width], scores[m][:].indirect(pos2_sb[:, c // 16 : (c + width) // 16]),
                    arrival[m][:, c : c + width], ALU.mult,
                )
                nc.sync.dma_start(out=out[m * P : (m + 1) * P, c : c + width], in_=res[:, c : c + width])

        make_scores(0)
        make_scores(1)
        pick_first(0)
        for m in range(MT):
            if m + 2 < MT:
                if m % 2 == 0:
                    gather_v2(m // 2 + 1)
                make_scores(m + 2)
            if m + 1 < MT:
                pick_first(m + 1)
            pick_second(m)
